import numpy as np
import ml_dtypes


def mxq(x, axis, fmt="e4m3"):
    dtype, down = {"e4m3": (ml_dtypes.float8_e4m3fn, 7), "e5m2": (ml_dtypes.float8_e5m2, 14)}[fmt]
    v = np.moveaxis(np.asarray(x, np.float32).astype(ml_dtypes.bfloat16).astype(np.float64), axis, -1)
    blocks = v.reshape(v.shape[:-1] + (-1, 32))
    amax = np.abs(blocks).max(-1, keepdims=True)
    byte = np.maximum(np.where(amax > 0, np.frexp(amax)[1] - 1 + 127, 0) - down, 1)
    scale = np.exp2(byte - 127.0)
    codes = (blocks / scale).astype(np.float32).astype(dtype).astype(np.float64)
    return np.moveaxis((codes * scale).reshape(v.shape), -1, axis)


WIDE = False


def mx_kscale(k):
    if not WIDE:
        return np.ones(k)
    levels = np.array([24, -24, 12, -12, 0])
    if k % 512:
        return np.exp2(np.random.permutation(np.resize(levels, k // 32))).repeat(32)
    a = np.empty((k // 512, 16))
    for p in range(k // 512):
        a[p, :8] = np.random.permutation(np.resize(levels, 8))
        for g in range(8):
            far = levels[np.abs(levels - a[p, g]) >= 10]
            a[p, g + 8] = far[np.random.randint(len(far))]
    return np.exp2(a.ravel()).repeat(32)


def f64(x):
    return np.asarray(x).astype(np.float64)


def striped8(idx):
    return np.concatenate([v.reshape(-1, 16).T for v in idx]).astype(np.uint16)


def unstriped8(offs):
    return np.stack([offs[16 * g:16 * g + 16].T.reshape(-1) for g in range(8)]).astype(np.int64)


E2M1 = np.array([0.0, 0.5, 1.0, 1.5, 2.0, 3.0, 4.0, 6.0, -0.0, -0.5, -1.0, -1.5, -2.0, -3.0, -4.0, -6.0])


def pack_weight(w, fmt):
    k, n = w.shape
    w = f64(np.asarray(w, np.float32).astype(ml_dtypes.bfloat16)).reshape(k // 32, 32, n)
    amax = np.abs(w).max(1)
    if fmt == "e4m3":
        byte = np.frexp(amax)[1] - 1 + 127 - 7
    else:
        mant, ex = np.frexp(amax / 6.0)
        byte = np.where(mant > 0.5, ex, ex - 1) + 127
    byte = np.clip(np.where(amax > 0, byte, 1), 1, 254)
    scaled = (w * np.exp2(127.0 - byte)[:, None, :]).reshape(k, n).astype(np.float32)
    by_word = np.ascontiguousarray(scaled.reshape(k // 512, 128, 4, n).transpose(0, 1, 3, 2))
    if fmt == "e4m3":
        words = by_word.astype(ml_dtypes.float8_e4m3fn).view(np.uint8)
    else:
        c = by_word.astype(ml_dtypes.float4_e2m1fn).view(np.uint8) & 0xF
        words = (c[..., 0::2] | (c[..., 1::2] << 4)).reshape(k // 512, 128, 2 * n)
    return np.ascontiguousarray(words), np.ascontiguousarray(byte.astype(np.uint8).reshape(k // 512, 16, n))


def unpack_weight(words, scales, fmt):
    g, _, n = scales.shape
    words = np.ascontiguousarray(words).reshape(g, 128, n, -1)
    if fmt == "e4m3":
        vals = words.view(ml_dtypes.float8_e4m3fn).astype(np.float64)
    else:
        nib = np.empty((g, 128, n, 4), np.uint8)
        nib[..., 0::2] = words & 0xF
        nib[..., 1::2] = words >> 4
        vals = E2M1[nib]
    vals = vals * np.repeat(np.exp2(scales.astype(np.float64) - 127.0), 8, axis=1)[..., None]
    return vals.transpose(0, 1, 3, 2).reshape(g * 512, n)


def planes(y):
    n, m = y.shape
    v = y.astype(np.float32).astype(ml_dtypes.bfloat16).astype(np.float64).reshape(n // 32, 32, m)
    top = np.abs(v).max(1)
    byte = np.clip(np.where(top > 0, np.frexp(top)[1] - 1 + 127 - 7, 1), 1, 254)
    codes = (v * np.exp2(127.0 - byte)[:, None, :]).reshape(n, m).astype(np.float32).astype(ml_dtypes.float8_e4m3fn).view(np.uint8)
    words = codes.reshape(n // 512, 128, 4, m).transpose(0, 1, 3, 2)
    return np.ascontiguousarray(words), np.ascontiguousarray(byte.astype(np.uint8).reshape(n // 512, 16, m))


def sigm(f):
    return 1.0 / (1.0 + np.exp(-np.maximum(f, -700.0)))


K, L, N, T, J = 512, 512, 512, 2048, 1024


def setup_inputs():
    n = np.random.standard_normal
    s = mx_kscale(K)[:, None]
    s2 = mx_kscale(L)[:, None]
    p_wa = pack_weight(n((K, N)) / np.sqrt(K) / s, "e2m1")
    p_wb = pack_weight(n((L, N)) / np.sqrt(L) / s2, "e2m1")
    return {
        "xT": (n((K, T)) * s).astype(np.float32),
        "wgt": np.repeat(np.random.uniform(0.5, 2.0, (8, J)), 16, axis=0).astype(np.float32),
        "zT": (n((L, T)) * s2).astype(np.float32),
        "wgt2": np.repeat(np.random.uniform(0.5, 2.0, (8, J)), 16, axis=0).astype(np.float32),
        "wa_words": p_wa[0],
        "wa_scales": p_wa[1],
        "wb_words": p_wb[0],
        "wb_scales": p_wb[1],
        "b": (0.3 * n(N)).astype(np.float32),
        "offs": striped8(np.stack([np.random.permutation(T)[:J] for _ in range(8)])),
        "offs2": striped8(np.stack([np.random.permutation(T)[:J] for _ in range(8)])),
    }


def reference(xT, wgt, zT, wgt2, wa_words, wa_scales, wb_words, wb_scales, b, offs, offs2):
    idx = unstriped8(offs)
    idx2 = unstriped8(offs2)
    rows = np.arange(K)
    xg = f64(wgt)[rows // 4 % 128] * f64(xT)[rows[:, None], idx[rows % 512 // 64]]
    xT_ = mxq(xg, 0, "e4m3")
    rows = np.arange(L)
    xg = f64(wgt2)[rows // 4 % 128] * f64(zT)[rows[:, None], idx2[rows % 512 // 64]]
    zT_ = mxq(xg, 0, "e4m3")
    wa_ = unpack_weight(wa_words, wa_scales, "e2m1")
    wb_ = unpack_weight(wb_words, wb_scales, "e2m1")
    ya = wa_.T @ xT_
    yb = wb_.T @ zT_
    out_0 = ya * sigm(yb) + f64(b)[:, None]
    return (out_0,) + planes(out_0)

@@ -1,0 +1,167 @@
+from contextlib import ExitStack
+
+import concourse.mybir as mybir
+
+K, N, T, J = 512, 512, 2048, 1024
+FLOPS = 2 * 2 * K * N * J
+
+F32 = mybir.dt.float32
+BF16 = mybir.dt.bfloat16
+I32 = mybir.dt.int32
+U32 = mybir.dt.uint32
+U16 = mybir.dt.uint16
+U8 = mybir.dt.uint8
+FP8X4 = mybir.dt.float8_e4m3fn_x4
+FP4X4 = mybir.dt.float4_e2m1fn_x4
+MULT = mybir.AluOpType.mult
+ACT = mybir.ActivationFunctionType
+
+P = 128
+PACK = 4
+C = 256
+CHUNKS = J // C
+
+
+def tile_list_gate_biasP_kernel(
+    tc, xT, wgt, zT, wgt2, wa_words, wa_scales, wb_words, wb_scales, b, offs, offs2, out_0, out_1, out_2
+):
+    nc = tc.nc
+    with ExitStack() as ctx:
+        keep = ctx.enter_context(tc.tile_pool(name="keep", bufs=1))
+        psum = ctx.enter_context(tc.psum_pool(name="psum", bufs=8))
+
+        def sb(name, shape, dtype):
+            return keep.tile(shape, dtype, name=name, align_bytes=64)
+
+        x_list = keep.tile([P, J // 16], U16, name="x_list")
+        z_list = keep.tile([P, J // 16], U16, name="z_list")
+        x_wgt = sb("x_wgt", [P, J], F32)
+        z_wgt = sb("z_wgt", [P, J], F32)
+        x_rows = [sb("x_rows%d" % i, [P, T], F32) for i in range(PACK)]
+        z_rows = [sb("z_rows%d" % i, [P, T], F32) for i in range(PACK)]
+        xv = xT.rearrange("(p i) t -> i p t", i=PACK)
+        zv = zT.rearrange("(p i) t -> i p t", i=PACK)
+        bias = sb("bias", [P, PACK], F32)
+
+        def load_weight(queue, name, words, scales):
+            raw_words = sb(name + "_raw_words", [P, 2 * N], U8)
+            raw_scales = sb(name + "_raw_scales", [P, N], U8)
+            nc.vector.memset(raw_scales[:].bitcast(I32), 0)
+            queue.dma_start(raw_words[:].bitcast(I32), words[0].bitcast(I32))
+            for q in range(4):
+                queue.dma_start(raw_scales[32 * q : 32 * q + 4, :].bitcast(I32), scales[0, 4 * q : 4 * q + 4, :].bitcast(I32))
+            return raw_words, raw_scales
+
+        def deal_weight(name, raw_words, raw_scales):
+            words = sb(name + "_words", [P, 2 * N], U8)
+            scales = sb(name + "_scales", [P, N], U8)
+            nc.vector.tensor_copy(
+                words[:].bitcast(U16).rearrange("p (i m) -> p i m", i=PACK),
+                raw_words[:].bitcast(U16).rearrange("p (m i) -> p i m", i=PACK),
+            )
+            nc.vector.tensor_copy(
+                scales[:].rearrange("p (i m) -> p i m", i=PACK), raw_scales[:].rearrange("p (m i) -> p i m", i=PACK)
+            )
+            return words, scales
+
+
+        nc.sync.dma_start(z_rows[0][:], zv[0])
+        nc.sync.dma_start(z_list[:], offs2)
+        nc.sync.dma_start(z_wgt[:, : J // 2], wgt2[:, : J // 2])
+        wb_raw = load_weight(nc.scalar, "wb", wb_words, wb_scales)
+        nc.sync.dma_start(z_wgt[:, J // 2 :], wgt2[:, J // 2 :])
+        for i in range(1, PACK):
+            nc.sync.dma_start(z_rows[i][:], zv[i])
+        nc.sync.dma_start(x_list[:], offs)
+        nc.sync.dma_start(x_wgt[:], wgt)
+        nc.sync.dma_start(x_rows[0][:], xv[0])
+        wa_raw = load_weight(nc.sync, "wa", wa_words, wa_scales)
+        nc.sync.dma_start(bias[:], b.rearrange("(p i) -> p i", i=PACK))
+        for i in range(1, PACK):
+            nc.sync.dma_start(x_rows[i][:], xv[i])
+        wb = deal_weight("wb", *wb_raw)
+
+        def gather(dst, rows, offsets, weights, j0, j1):
+            nc.vector.tensor_tensor(dst, rows[:].indirect(offsets[:, j0 // 16 : j1 // 16]), weights[:, j0:j1], MULT)
+
+        def weave(engine_copy, dst, src):
+            engine_copy(
+                dst[:].rearrange("p (c u i) -> p c i u", u=4, i=PACK),
+                src.rearrange("p i (c u) -> p c i u", u=4),
+            )
+
+        def weave_pair(engine_copy, dst, src, h):
+            engine_copy(
+                dst[:].rearrange("p (c u i) -> p c i u", u=4, i=PACK)[:, :, 2 * h : 2 * h + 2, :],
+                src.rearrange("p i (c u) -> p c i u", u=4),
+            )
+
+        def project(weight, name, picked):
+            w_words, w_scales = weight
+            codes = sb(name + "_codes", [P, C], U32)
+            scales = sb(name + "_scales", [P, C], U8)
+            nc.vector.quantize_mx(out=codes[:].bitcast(FP8X4), scales=scales[:], in_=picked[:])
+            banks = []
+            for h in range(2):
+                bank = psum.tile([P, 2, C], F32, name="bank")
+                for e in range(2):
+                    col = P * (2 * h + e)
+                    nc.tensor.matmul_mx(
+                        out=bank[:, e, :],
+                        lhsT=w_words[:, 2 * col : 2 * (col + P)].bitcast(FP4X4),
+                        lhsT_scale=w_scales[:, col : col + P],
+                        rhs=codes[:].bitcast(FP8X4),
+                        rhs_scale=scales[:],
+                        start=True,
+                        stop=True,
+                    )
+                banks.append(bank)
+            return banks
+
+        zg = [[sb("zg%d_%d" % (h, c), [P, 2, C], F32) for c in range(CHUNKS)] for h in range(2)]
+        zb = [sb("zb%d" % c, [P, PACK * C], BF16) for c in range(CHUNKS)]
+        xg = [sb("xg%d" % c, [P, PACK, C], F32) for c in range(CHUNKS)]
+        gate = []
+        for h in range(2):
+            for e in range(2):
+                for c in range(CHUNKS):
+                    gather(zg[h][c][:, e, :], z_rows[2 * h + e], z_list, z_wgt, C * c, C * (c + 1))
+            for c in range(CHUNKS):
+                weave_pair(nc.scalar.copy, zb[c], zg[h][c][:], h)
+        for c in range(CHUNKS):
+            banks = project(wb, "z%d" % c, zb[c])
+            g = sb("gate%d" % c, [P, PACK, C], F32)
+            for h in range(2):
+                nc.scalar.activation(g[:, 2 * h : 2 * h + 2, :], banks[h][:], ACT.Sigmoid)
+            gate.append(g)
+
+        wa = deal_weight("wa", *wa_raw)
+        for i in range(PACK):
+            for c in range(CHUNKS):
+                gather(xg[c][:, i, :], x_rows[i], x_list, x_wgt, C * c, C * (c + 1))
+
+        y_scales = sb("y_scales", [P, J], U8)
+        ov = out_0.rearrange("(p i) j -> p i j", i=PACK)
+        for c in range(CHUNKS):
+            cols = slice(C * c, C * (c + 1))
+            xb = sb("xb%d" % c, [P, PACK * C], BF16)
+            weave(nc.scalar.copy, xb, xg[c][:])
+            banks = project(wa, "x%d" % c, xb)
+            prod = sb("prod%d" % c, [P, PACK, C], F32)
+            for h in range(2):
+                nc.vector.tensor_tensor(prod[:, 2 * h : 2 * h + 2, :], banks[h][:], gate[c][:, 2 * h : 2 * h + 2, :], MULT)
+            y = sb("y%d" % c, [P, PACK, C], F32)
+            for i in range(PACK):
+                nc.scalar.activation(y[:, i, :], prod[:, i, :], ACT.Identity, bias=bias[:, i : i + 1])
+            nc.sync.dma_start(ov[:, :, cols], y[:])
+            yb = sb("yb%d" % c, [P, PACK * C], BF16)
+            weave(nc.vector.tensor_copy, yb, y[:])
+            y_codes = sb("y_codes%d" % c, [P, C], U32)
+            nc.vector.quantize_mx(out=y_codes[:].bitcast(FP8X4), scales=y_scales[:, cols], in_=yb[:])
+            nc.sync.dma_start(
+                out_1[0].rearrange("p j i -> p (j i)")[:, PACK * C * c : PACK * C * (c + 1)].bitcast(I32),
+                y_codes[:].bitcast(I32),
+            )
+        for q in range(4):
+            queue = nc.sync if q % 2 == 0 else nc.scalar
+            queue.dma_start(out_2[0, 4 * q : 4 * q + 4, :].bitcast(I32), y_scales[32 * q : 32 * q + 4, :].bitcast(I32))

@@ -20,6 +20,9 @@ P = 128
 PACK = 4
 C = 256
 CHUNKS = J // C
+LATE = T - T // 8
+X_CUTS = (0, 256, 512, 768, 1024)
+WEAVE_ON_SCALAR = (0, 1, 2)
 
 
 def tile_list_gate_biasP_kernel(
@@ -64,21 +67,24 @@ def tile_list_gate_biasP_kernel(
             )
             return words, scales
 
-
+        warm = sb("warm", [P, 2], F32)
+        nc.vector.memset(warm[:, 0:1], 0.0)
+        nc.scalar.activation(warm[:, 1:2], warm[:, 0:1], ACT.Sigmoid)
         nc.sync.dma_start(z_rows[0][:], zv[0])
         nc.sync.dma_start(z_list[:], offs2)
-        nc.sync.dma_start(z_wgt[:, : J // 2], wgt2[:, : J // 2])
+        nc.sync.dma_start(z_wgt[:, :C], wgt2[:, :C])
         wb_raw = load_weight(nc.scalar, "wb", wb_words, wb_scales)
-        nc.sync.dma_start(z_wgt[:, J // 2 :], wgt2[:, J // 2 :])
+        nc.sync.dma_start(z_wgt[:, C:], wgt2[:, C:])
         for i in range(1, PACK):
             nc.sync.dma_start(z_rows[i][:], zv[i])
+        wa_raw = load_weight(nc.sync, "wa", wa_words, wa_scales)
         nc.sync.dma_start(x_list[:], offs)
         nc.sync.dma_start(x_wgt[:], wgt)
         nc.sync.dma_start(x_rows[0][:], xv[0])
-        wa_raw = load_weight(nc.sync, "wa", wa_words, wa_scales)
         nc.sync.dma_start(bias[:], b.rearrange("(p i) -> p i", i=PACK))
-        for i in range(1, PACK):
-            nc.sync.dma_start(x_rows[i][:], xv[i])
+        nc.sync.dma_start(x_rows[1][:], xv[1])
+        nc.sync.dma_start(x_rows[2][:], xv[2])
+        nc.sync.dma_start(x_rows[3][:], xv[3])
         wb = deal_weight("wb", *wb_raw)
 
         def gather(dst, rows, offsets, weights, j0, j1):
@@ -96,16 +102,17 @@ def tile_list_gate_biasP_kernel(
                 src.rearrange("p i (c u) -> p c i u", u=4),
             )
 
-        def project(weight, name, picked):
+        def project(weight, name, picked, C):
             w_words, w_scales = weight
             codes = sb(name + "_codes", [P, C], U32)
             scales = sb(name + "_scales", [P, C], U8)
             nc.vector.quantize_mx(out=codes[:].bitcast(FP8X4), scales=scales[:], in_=picked[:])
             banks = []
-            for h in range(2):
-                bank = psum.tile([P, 2, C], F32, name="bank")
-                for e in range(2):
-                    col = P * (2 * h + e)
+            per_bank = 512 // C
+            for h in range(PACK // per_bank):
+                bank = psum.tile([P, per_bank, C], F32, name="bank")
+                for e in range(per_bank):
+                    col = P * (per_bank * h + e)
                     nc.tensor.matmul_mx(
                         out=bank[:, e, :],
                         lhsT=w_words[:, 2 * col : 2 * (col + P)].bitcast(FP4X4),
@@ -118,48 +125,76 @@ def tile_list_gate_biasP_kernel(
                 banks.append(bank)
             return banks
 
-        zg = [[sb("zg%d_%d" % (h, c), [P, 2, C], F32) for c in range(CHUNKS)] for h in range(2)]
+        zg = [sb("zg%d" % h, [P, 2, J], F32) for h in range(2)]
         zb = [sb("zb%d" % c, [P, PACK * C], BF16) for c in range(CHUNKS)]
-        xg = [sb("xg%d" % c, [P, PACK, C], F32) for c in range(CHUNKS)]
         gate = []
-        for h in range(2):
-            for e in range(2):
-                for c in range(CHUNKS):
-                    gather(zg[h][c][:, e, :], z_rows[2 * h + e], z_list, z_wgt, C * c, C * (c + 1))
-            for c in range(CHUNKS):
-                weave_pair(nc.scalar.copy, zb[c], zg[h][c][:], h)
+        gather(zg[0][:, 0, :C], z_rows[0], z_list, z_wgt, 0, C)
+        gather(zg[0][:, 0, C:], z_rows[0], z_list, z_wgt, C, J)
+        gather(zg[0][:, 1, :], z_rows[1], z_list, z_wgt, 0, J)
         for c in range(CHUNKS):
-            banks = project(wb, "z%d" % c, zb[c])
+            weave_pair(nc.scalar.copy, zb[c], zg[0][:, :, C * c : C * (c + 1)], 0)
+        gather(zg[1][:, 0, :], z_rows[2], z_list, z_wgt, 0, J)
+        for c in range(CHUNKS):
+            gather(zg[1][:, 1, C * c : C * (c + 1)], z_rows[3], z_list, z_wgt, C * c, C * (c + 1))
+            weave_pair(nc.scalar.copy, zb[c], zg[1][:, :, C * c : C * (c + 1)], 1)
+        for c in range(CHUNKS):
+            banks = project(wb, "z%d" % c, zb[c], C)
             g = sb("gate%d" % c, [P, PACK, C], F32)
             for h in range(2):
                 nc.scalar.activation(g[:, 2 * h : 2 * h + 2, :], banks[h][:], ACT.Sigmoid)
             gate.append(g)
 
         wa = deal_weight("wa", *wa_raw)
-        for i in range(PACK):
-            for c in range(CHUNKS):
-                gather(xg[c][:, i, :], x_rows[i], x_list, x_wgt, C * c, C * (c + 1))
+        spans = list(zip(X_CUTS[:-1], X_CUTS[1:]))
+        xg = [sb("xg%d" % j0, [P, PACK + 1, j1 - j0], F32) for j0, j1 in spans]
+        for i in range(2):
+            for c, (j0, j1) in enumerate(spans):
+                gather(xg[c][:, i, :], x_rows[i], x_list, x_wgt, j0, j1)
+        late = {0: 2, 1: 2}
 
         y_scales = sb("y_scales", [P, J], U8)
         ov = out_0.rearrange("(p i) j -> p i j", i=PACK)
-        for c in range(CHUNKS):
-            cols = slice(C * c, C * (c + 1))
-            xb = sb("xb%d" % c, [P, PACK * C], BF16)
-            weave(nc.scalar.copy, xb, xg[c][:])
-            banks = project(wa, "x%d" % c, xb)
-            prod = sb("prod%d" % c, [P, PACK, C], F32)
-            for h in range(2):
-                nc.vector.tensor_tensor(prod[:, 2 * h : 2 * h + 2, :], banks[h][:], gate[c][:, 2 * h : 2 * h + 2, :], MULT)
-            y = sb("y%d" % c, [P, PACK, C], F32)
+        def pick(c):
+            j0, j1 = spans[c]
+            for i in range(2, PACK):
+                gather(xg[c][:, i, :], x_rows[i], x_list, x_wgt, j0, j1)
+
+        def stage1(c):
+            j0, j1 = spans[c]
+            if c in late:
+                xb = xg[c + 2][:, late[c] : late[c] + 2, :].rearrange("p i j -> p (i j)").bitcast(BF16)
+            else:
+                xb = sb("xb%d" % c, [P, PACK * (j1 - j0)], BF16)[:]
+            weave(nc.scalar.copy, xb, xg[c][:, :PACK, :])
+            banks = project(wa, "x%d" % c, xb, j1 - j0)
+            if c + 2 < len(spans):
+                pick(c + 2)
+            return banks
+
+        pick(0)
+        pick(1)
+        for c, (j0, j1) in enumerate(spans):
+            width = j1 - j0
+            cols = slice(j0, j1)
+            banks = stage1(c)
+            prod = sb("prod%d" % c, [P, PACK, width], F32)
+            per_bank = PACK // len(banks)
+            for h, bank in enumerate(banks):
+                rows = slice(per_bank * h, per_bank * (h + 1))
+                nc.vector.tensor_tensor(prod[:, rows, :], bank[:], gate[j0 // C][:, rows, j0 % C : j0 % C + width], MULT)
+            y = sb("y%d" % c, [P, PACK, width], F32)
             for i in range(PACK):
-                nc.scalar.activation(y[:, i, :], prod[:, i, :], ACT.Identity, bias=bias[:, i : i + 1])
+                if c in (3,):
+                    nc.vector.tensor_scalar_add(y[:, i, :], prod[:, i, :], bias[:, i : i + 1])
+                else:
+                    nc.scalar.activation(y[:, i, :], prod[:, i, :], ACT.Identity, bias=bias[:, i : i + 1])
             nc.sync.dma_start(ov[:, :, cols], y[:])
-            yb = sb("yb%d" % c, [P, PACK * C], BF16)
-            weave(nc.vector.tensor_copy, yb, y[:])
-            y_codes = sb("y_codes%d" % c, [P, C], U32)
+            yb = sb("yb%d" % c, [P, PACK * width], BF16)
+            weave(nc.scalar.copy if c in WEAVE_ON_SCALAR else nc.vector.tensor_copy, yb, y[:])
+            y_codes = sb("y_codes%d" % c, [P, width], U32)
             nc.vector.quantize_mx(out=y_codes[:].bitcast(FP8X4), scales=y_scales[:, cols], in_=yb[:])
             nc.sync.dma_start(
-                out_1[0].rearrange("p j i -> p (j i)")[:, PACK * C * c : PACK * C * (c + 1)].bitcast(I32),
+                out_1[0].rearrange("p j i -> p (j i)")[:, PACK * j0 : PACK * j1].bitcast(I32),
                 y_codes[:].bitcast(I32),
             )
         for q in range(4):

@@ -46,14 +46,19 @@ def tile_list_gate_biasP_kernel(
         zv = zT.rearrange("(p i) t -> i p t", i=PACK)
         bias = sb("bias", [P, PACK], F32)
 
-        def load_weight(queue, name, words, scales):
+        def cleared_plane(name):
+            plane = sb(name + "_raw_scales", [P, N], U8)
+            nc.gpsimd.memset(plane[:].bitcast(I32), 0)
+            return plane
+
+        def load_scales(plane, scales, quadrants):
+            for q in quadrants:
+                nc.sync.dma_start(plane[32 * q : 32 * q + 4, :].bitcast(I32), scales[0, 4 * q : 4 * q + 4, :].bitcast(I32))
+
+        def load_words(name, words):
             raw_words = sb(name + "_raw_words", [P, 2 * N], U8)
-            raw_scales = sb(name + "_raw_scales", [P, N], U8)
-            nc.vector.memset(raw_scales[:].bitcast(I32), 0)
-            queue.dma_start(raw_words[:].bitcast(I32), words[0].bitcast(I32))
-            for q in range(4):
-                queue.dma_start(raw_scales[32 * q : 32 * q + 4, :].bitcast(I32), scales[0, 4 * q : 4 * q + 4, :].bitcast(I32))
-            return raw_words, raw_scales
+            nc.sync.dma_start(raw_words[:].bitcast(I32), words[0].bitcast(I32))
+            return raw_words
 
         def deal_weight(name, raw_words, raw_scales):
             words = sb(name + "_words", [P, 2 * N], U8)
@@ -67,23 +72,28 @@ def tile_list_gate_biasP_kernel(
             )
             return words, scales
 
-        warm = sb("warm", [P, 2], F32)
-        nc.vector.memset(warm[:, 0:1], 0.0)
-        nc.scalar.activation(warm[:, 1:2], warm[:, 0:1], ACT.Sigmoid)
+
+        wb_plane = cleared_plane("wb")
+        wa_plane = cleared_plane("wa")
         nc.sync.dma_start(z_rows[0][:], zv[0])
         nc.sync.dma_start(z_list[:], offs2)
         nc.sync.dma_start(z_wgt[:, :C], wgt2[:, :C])
-        wb_raw = load_weight(nc.scalar, "wb", wb_words, wb_scales)
         nc.sync.dma_start(z_wgt[:, C:], wgt2[:, C:])
-        for i in range(1, PACK):
-            nc.sync.dma_start(z_rows[i][:], zv[i])
-        wa_raw = load_weight(nc.sync, "wa", wa_words, wa_scales)
+        nc.sync.dma_start(z_rows[1][:], zv[1])
+        wb_raw = load_words("wb", wb_words), wb_plane
+        load_scales(wb_plane, wb_scales, (0, 1))
+        nc.sync.dma_start(z_rows[2][:], zv[2])
+        load_scales(wb_plane, wb_scales, (2, 3))
+        nc.sync.dma_start(z_rows[3][:], zv[3])
         nc.sync.dma_start(x_list[:], offs)
         nc.sync.dma_start(x_wgt[:], wgt)
         nc.sync.dma_start(x_rows[0][:], xv[0])
-        nc.sync.dma_start(bias[:], b.rearrange("(p i) -> p i", i=PACK))
+        wa_raw = load_words("wa", wa_words), wa_plane
+        load_scales(wa_plane, wa_scales, (0, 1))
         nc.sync.dma_start(x_rows[1][:], xv[1])
+        load_scales(wa_plane, wa_scales, (2, 3))
         nc.sync.dma_start(x_rows[2][:], xv[2])
+        nc.sync.dma_start(bias[:], b.rearrange("(p i) -> p i", i=PACK))
         nc.sync.dma_start(x_rows[3][:], xv[3])
         wb = deal_weight("wb", *wb_raw)
 
@@ -102,9 +112,9 @@ def tile_list_gate_biasP_kernel(
                 src.rearrange("p i (c u) -> p c i u", u=4),
             )
 
-        def project(weight, name, picked, C):
+        def project(weight, name, picked, C, tag=None):
             w_words, w_scales = weight
-            codes = sb(name + "_codes", [P, C], U32)
+            codes = keep.tile([P, C], U32, name=name + "_codes", tag=tag or name + "_codes", align_bytes=64)
             scales = sb(name + "_scales", [P, C], U8)
             nc.vector.quantize_mx(out=codes[:].bitcast(FP8X4), scales=scales[:], in_=picked[:])
             banks = []
@@ -126,7 +136,8 @@ def tile_list_gate_biasP_kernel(
             return banks
 
         zg = [sb("zg%d" % h, [P, 2, J], F32) for h in range(2)]
-        zb = [sb("zb%d" % c, [P, PACK * C], BF16) for c in range(CHUNKS)]
+        z_half = [sb("z_half%d" % h, [P, 2 * PACK * C], BF16) for h in range(2)]
+        zb = [z_half[c // 2][:, PACK * C * (c % 2) : PACK * C * (c % 2 + 1)] for c in range(CHUNKS)]
         gate = []
         gather(zg[0][:, 0, :C], z_rows[0], z_list, z_wgt, 0, C)
         gather(zg[0][:, 0, C:], z_rows[0], z_list, z_wgt, C, J)
@@ -137,19 +148,21 @@ def tile_list_gate_biasP_kernel(
         for c in range(CHUNKS):
             gather(zg[1][:, 1, C * c : C * (c + 1)], z_rows[3], z_list, z_wgt, C * c, C * (c + 1))
             weave_pair(nc.scalar.copy, zb[c], zg[1][:, :, C * c : C * (c + 1)], 1)
-        for c in range(CHUNKS):
-            banks = project(wb, "z%d" % c, zb[c], C)
-            g = sb("gate%d" % c, [P, PACK, C], F32)
-            for h in range(2):
-                nc.scalar.activation(g[:, 2 * h : 2 * h + 2, :], banks[h][:], ACT.Sigmoid)
+        def open_gate(h, tag):
+            g = sb("gate%d" % h, [P, PACK, 2 * C], F32)
+            for e, bank in enumerate(project(wb, "z%d" % h, z_half[h], 2 * C, tag)):
+                nc.scalar.activation(g[:, e, :], bank[:, 0, :], ACT.Sigmoid)
             gate.append(g)
 
+        open_gate(0, None)
         wa = deal_weight("wa", *wa_raw)
         spans = list(zip(X_CUTS[:-1], X_CUTS[1:]))
-        xg = [sb("xg%d" % j0, [P, PACK + 1, j1 - j0], F32) for j0, j1 in spans]
+        xg = [sb("xg%d" % j0, [P, PACK + 2, j1 - j0], F32) for j0, j1 in spans]
         for i in range(2):
             for c, (j0, j1) in enumerate(spans):
                 gather(xg[c][:, i, :], x_rows[i], x_list, x_wgt, j0, j1)
+            if i == 0:
+                open_gate(1, "x_rows0")
         late = {0: 2, 1: 2}
 
         y_scales = sb("y_scales", [P, J], U8)
@@ -162,7 +175,7 @@ def tile_list_gate_biasP_kernel(
         def stage1(c):
             j0, j1 = spans[c]
             if c in late:
-                xb = xg[c + 2][:, late[c] : late[c] + 2, :].rearrange("p i j -> p (i j)").bitcast(BF16)
+                xb = xg[c + 2][:, late[c] :, :].rearrange("p i j -> p (i j)")[:, : 2 * (j1 - j0)].bitcast(BF16)
             else:
                 xb = sb("xb%d" % c, [P, PACK * (j1 - j0)], BF16)[:]
             weave(nc.scalar.copy, xb, xg[c][:, :PACK, :])
@@ -181,7 +194,7 @@ def tile_list_gate_biasP_kernel(
             per_bank = PACK // len(banks)
             for h, bank in enumerate(banks):
                 rows = slice(per_bank * h, per_bank * (h + 1))
-                nc.vector.tensor_tensor(prod[:, rows, :], bank[:], gate[j0 // C][:, rows, j0 % C : j0 % C + width], MULT)
+                nc.vector.tensor_tensor(prod[:, rows, :], bank[:], gate[j0 // (2 * C)][:, rows, j0 % (2 * C) : j0 % (2 * C) + width], MULT)
             y = sb("y%d" % c, [P, PACK, width], F32)
             for i in range(PACK):
                 if c in (3,):

@@ -17,12 +17,18 @@ MULT = mybir.AluOpType.mult
 ACT = mybir.ActivationFunctionType
 
 P = 128
-PACK = 4
-C = 256
-CHUNKS = J // C
-LATE = T - T // 8
-X_CUTS = (0, 256, 512, 768, 1024)
-WEAVE_ON_SCALAR = (0, 1, 2)
+PLANES = 4
+LIST_ROWS = 16
+QUADRANTS = 4
+BANKS = 8
+BANK_COLS = 512
+RUN = 4
+CHUNK = 256
+CHUNKS = J // CHUNK
+HALF = J // 2
+LAST = CHUNKS - 1
+Y_WOVEN_ON_VECTOR = (0, LAST)
+BIAS_ON_VECTOR = (LAST,)
 
 
 def tile_list_gate_biasP_kernel(
@@ -31,98 +37,97 @@ def tile_list_gate_biasP_kernel(
     nc = tc.nc
     with ExitStack() as ctx:
         keep = ctx.enter_context(tc.tile_pool(name="keep", bufs=1))
-        psum = ctx.enter_context(tc.psum_pool(name="psum", bufs=8))
+        psum = ctx.enter_context(tc.psum_pool(name="psum", bufs=BANKS))
 
-        def sb(name, shape, dtype):
-            return keep.tile(shape, dtype, name=name, align_bytes=64)
+        def sb(name, shape, dtype, tag=None):
+            return keep.tile(shape, dtype, name=name, tag=tag or name, align_bytes=64)
 
-        x_list = keep.tile([P, J // 16], U16, name="x_list")
-        z_list = keep.tile([P, J // 16], U16, name="z_list")
+        x_list = keep.tile([P, J // LIST_ROWS], U16, name="x_list")
+        z_list = keep.tile([P, J // LIST_ROWS], U16, name="z_list")
         x_wgt = sb("x_wgt", [P, J], F32)
         z_wgt = sb("z_wgt", [P, J], F32)
-        x_rows = [sb("x_rows%d" % i, [P, T], F32) for i in range(PACK)]
-        z_rows = [sb("z_rows%d" % i, [P, T], F32) for i in range(PACK)]
-        xv = xT.rearrange("(p i) t -> i p t", i=PACK)
-        zv = zT.rearrange("(p i) t -> i p t", i=PACK)
-        bias = sb("bias", [P, PACK], F32)
+        x_planes = [sb("x_plane%d" % i, [P, T], F32) for i in range(PLANES)]
+        z_planes = [sb("z_plane%d" % i, [P, T], F32) for i in range(PLANES)]
+        x_hbm = xT.rearrange("(p i) t -> i p t", i=PLANES)
+        z_hbm = zT.rearrange("(p i) t -> i p t", i=PLANES)
+        bias = sb("bias", [P, PLANES], F32)
 
-        def cleared_plane(name):
-            plane = sb(name + "_raw_scales", [P, N], U8)
-            nc.gpsimd.memset(plane[:].bitcast(I32), 0)
-            return plane
+        def cleared_scale_tile(name):
+            scale_tile = sb(name, [P, N], U8)
+            nc.gpsimd.memset(scale_tile[:].bitcast(I32), 0)
+            return scale_tile
 
-        def load_scales(plane, scales, quadrants):
+        def load_scales(scale_tile, scales, quadrants):
             for q in quadrants:
-                nc.sync.dma_start(plane[32 * q : 32 * q + 4, :].bitcast(I32), scales[0, 4 * q : 4 * q + 4, :].bitcast(I32))
+                nc.sync.dma_start(
+                    scale_tile[32 * q : 32 * q + 4, :].bitcast(I32), scales[0, 4 * q : 4 * q + 4, :].bitcast(I32)
+                )
 
         def load_words(name, words):
-            raw_words = sb(name + "_raw_words", [P, 2 * N], U8)
-            nc.sync.dma_start(raw_words[:].bitcast(I32), words[0].bitcast(I32))
-            return raw_words
+            word_tile = sb(name, [P, 2 * N], U8)
+            nc.sync.dma_start(word_tile[:].bitcast(I32), words[0].bitcast(I32))
+            return word_tile
 
-        def deal_weight(name, raw_words, raw_scales):
+        def deal_weight(name, word_tile, scale_tile):
             words = sb(name + "_words", [P, 2 * N], U8)
             scales = sb(name + "_scales", [P, N], U8)
             nc.vector.tensor_copy(
-                words[:].bitcast(U16).rearrange("p (i m) -> p i m", i=PACK),
-                raw_words[:].bitcast(U16).rearrange("p (m i) -> p i m", i=PACK),
+                words[:].bitcast(U16).rearrange("p (i m) -> p i m", i=PLANES),
+                word_tile[:].bitcast(U16).rearrange("p (m i) -> p i m", i=PLANES),
             )
             nc.vector.tensor_copy(
-                scales[:].rearrange("p (i m) -> p i m", i=PACK), raw_scales[:].rearrange("p (m i) -> p i m", i=PACK)
+                scales[:].rearrange("p (i m) -> p i m", i=PLANES), scale_tile[:].rearrange("p (m i) -> p i m", i=PLANES)
             )
             return words, scales
 
-
-        wb_plane = cleared_plane("wb")
-        wa_plane = cleared_plane("wa")
-        nc.sync.dma_start(z_rows[0][:], zv[0])
+        wb_scale_tile = cleared_scale_tile("wb_loaded_scales")
+        wa_scale_tile = cleared_scale_tile("wa_loaded_scales")
+        nc.sync.dma_start(z_planes[0][:], z_hbm[0])
         nc.sync.dma_start(z_list[:], offs2)
-        nc.sync.dma_start(z_wgt[:, :C], wgt2[:, :C])
-        nc.sync.dma_start(z_wgt[:, C:], wgt2[:, C:])
-        nc.sync.dma_start(z_rows[1][:], zv[1])
-        wb_raw = load_words("wb", wb_words), wb_plane
-        load_scales(wb_plane, wb_scales, (0, 1))
-        nc.sync.dma_start(z_rows[2][:], zv[2])
-        load_scales(wb_plane, wb_scales, (2, 3))
-        nc.sync.dma_start(z_rows[3][:], zv[3])
+        nc.sync.dma_start(z_wgt[:, :CHUNK], wgt2[:, :CHUNK])
+        nc.sync.dma_start(z_wgt[:, CHUNK:], wgt2[:, CHUNK:])
+        nc.sync.dma_start(z_planes[1][:], z_hbm[1])
+        wb_word_tile = load_words("wb_loaded_words", wb_words)
+        load_scales(wb_scale_tile, wb_scales, (0, 1))
+        nc.sync.dma_start(z_planes[2][:], z_hbm[2])
+        load_scales(wb_scale_tile, wb_scales, (2, 3))
+        nc.sync.dma_start(z_planes[3][:], z_hbm[3])
         nc.sync.dma_start(x_list[:], offs)
         nc.sync.dma_start(x_wgt[:], wgt)
-        nc.sync.dma_start(x_rows[0][:], xv[0])
-        wa_raw = load_words("wa", wa_words), wa_plane
-        load_scales(wa_plane, wa_scales, (0, 1))
-        nc.sync.dma_start(x_rows[1][:], xv[1])
-        load_scales(wa_plane, wa_scales, (2, 3))
-        nc.sync.dma_start(x_rows[2][:], xv[2])
-        nc.sync.dma_start(bias[:], b.rearrange("(p i) -> p i", i=PACK))
-        nc.sync.dma_start(x_rows[3][:], xv[3])
-        wb = deal_weight("wb", *wb_raw)
+        nc.sync.dma_start(x_planes[0][:], x_hbm[0])
+        wa_word_tile = load_words("wa_loaded_words", wa_words)
+        load_scales(wa_scale_tile, wa_scales, (0, 1))
+        nc.sync.dma_start(x_planes[1][:], x_hbm[1])
+        load_scales(wa_scale_tile, wa_scales, (2, 3))
+        nc.sync.dma_start(x_planes[2][:], x_hbm[2])
+        nc.sync.dma_start(bias[:], b.rearrange("(p i) -> p i", i=PLANES))
+        nc.sync.dma_start(x_planes[3][:], x_hbm[3])
+        wb = deal_weight("wb", wb_word_tile, wb_scale_tile)
 
-        def gather(dst, rows, offsets, weights, j0, j1):
-            nc.vector.tensor_tensor(dst, rows[:].indirect(offsets[:, j0 // 16 : j1 // 16]), weights[:, j0:j1], MULT)
+        def chunk_cols(c):
+            return slice(CHUNK * c, CHUNK * (c + 1))
 
-        def weave(engine_copy, dst, src):
+        def gather(dst, plane, offsets, weights, cols):
+            picked = plane[:].indirect(offsets[:, cols.start // LIST_ROWS : cols.stop // LIST_ROWS])
+            nc.vector.tensor_tensor(dst, picked, weights[:, cols], MULT)
+
+        def weave(engine_copy, dst, src, planes=slice(0, PLANES)):
             engine_copy(
-                dst[:].rearrange("p (c u i) -> p c i u", u=4, i=PACK),
-                src.rearrange("p i (c u) -> p c i u", u=4),
+                dst.rearrange("p (c u i) -> p c i u", u=RUN, i=PLANES)[:, :, planes, :],
+                src.rearrange("p i (c u) -> p c i u", u=RUN),
             )
 
-        def weave_pair(engine_copy, dst, src, h):
-            engine_copy(
-                dst[:].rearrange("p (c u i) -> p c i u", u=4, i=PACK)[:, :, 2 * h : 2 * h + 2, :],
-                src.rearrange("p i (c u) -> p c i u", u=4),
-            )
-
-        def project(weight, name, picked, C, tag=None):
+        def project(weight, name, woven, width, codes_tag=None):
             w_words, w_scales = weight
-            codes = keep.tile([P, C], U32, name=name + "_codes", tag=tag or name + "_codes", align_bytes=64)
-            scales = sb(name + "_scales", [P, C], U8)
-            nc.vector.quantize_mx(out=codes[:].bitcast(FP8X4), scales=scales[:], in_=picked[:])
+            codes = sb(name + "_codes", [P, width], U32, codes_tag)
+            scales = sb(name + "_scales", [P, width], U8)
+            nc.vector.quantize_mx(out=codes[:].bitcast(FP8X4), scales=scales[:], in_=woven)
             banks = []
-            per_bank = 512 // C
-            for h in range(PACK // per_bank):
-                bank = psum.tile([P, per_bank, C], F32, name="bank")
+            per_bank = BANK_COLS // width
+            for first in range(0, PLANES, per_bank):
+                bank = psum.tile([P, per_bank, width], F32, name="bank")
                 for e in range(per_bank):
-                    col = P * (per_bank * h + e)
+                    col = P * (first + e)
                     nc.tensor.matmul_mx(
                         out=bank[:, e, :],
                         lhsT=w_words[:, 2 * col : 2 * (col + P)].bitcast(FP4X4),
@@ -135,81 +140,82 @@ def tile_list_gate_biasP_kernel(
                 banks.append(bank)
             return banks
 
-        zg = [sb("zg%d" % h, [P, 2, J], F32) for h in range(2)]
-        z_half = [sb("z_half%d" % h, [P, 2 * PACK * C], BF16) for h in range(2)]
-        zb = [z_half[c // 2][:, PACK * C * (c % 2) : PACK * C * (c % 2 + 1)] for c in range(CHUNKS)]
-        gate = []
-        gather(zg[0][:, 0, :C], z_rows[0], z_list, z_wgt, 0, C)
-        gather(zg[0][:, 0, C:], z_rows[0], z_list, z_wgt, C, J)
-        gather(zg[0][:, 1, :], z_rows[1], z_list, z_wgt, 0, J)
-        for c in range(CHUNKS):
-            weave_pair(nc.scalar.copy, zb[c], zg[0][:, :, C * c : C * (c + 1)], 0)
-        gather(zg[1][:, 0, :], z_rows[2], z_list, z_wgt, 0, J)
-        for c in range(CHUNKS):
-            gather(zg[1][:, 1, C * c : C * (c + 1)], z_rows[3], z_list, z_wgt, C * c, C * (c + 1))
-            weave_pair(nc.scalar.copy, zb[c], zg[1][:, :, C * c : C * (c + 1)], 1)
-        def open_gate(h, tag):
-            g = sb("gate%d" % h, [P, PACK, 2 * C], F32)
-            for e, bank in enumerate(project(wb, "z%d" % h, z_half[h], 2 * C, tag)):
-                nc.scalar.activation(g[:, e, :], bank[:, 0, :], ACT.Sigmoid)
-            gate.append(g)
+        z_pairs = [sb("z_pair%d" % h, [P, 2, J], F32) for h in range(2)]
+        z_woven = [sb("z_woven%d" % h, [P, PLANES * HALF], BF16) for h in range(2)]
 
-        open_gate(0, None)
-        wa = deal_weight("wa", *wa_raw)
-        spans = list(zip(X_CUTS[:-1], X_CUTS[1:]))
-        xg = [sb("xg%d" % j0, [P, PACK + 2, j1 - j0], F32) for j0, j1 in spans]
-        for i in range(2):
-            for c, (j0, j1) in enumerate(spans):
-                gather(xg[c][:, i, :], x_rows[i], x_list, x_wgt, j0, j1)
-            if i == 0:
-                open_gate(1, "x_rows0")
-        late = {0: 2, 1: 2}
+        def weave_z_pair(pair, c):
+            start = PLANES * (CHUNK * c % HALF)
+            dst = z_woven[CHUNK * c // HALF][:, start : start + PLANES * CHUNK]
+            weave(nc.scalar.copy, dst, z_pairs[pair][:, :, chunk_cols(c)], slice(2 * pair, 2 * pair + 2))
+
+        gather(z_pairs[0][:, 0, :CHUNK], z_planes[0], z_list, z_wgt, slice(0, CHUNK))
+        gather(z_pairs[0][:, 0, CHUNK:], z_planes[0], z_list, z_wgt, slice(CHUNK, J))
+        gather(z_pairs[0][:, 1, :], z_planes[1], z_list, z_wgt, slice(0, J))
+        for c in range(CHUNKS):
+            weave_z_pair(0, c)
+        gather(z_pairs[1][:, 0, :], z_planes[2], z_list, z_wgt, slice(0, J))
+        for c in range(CHUNKS):
+            gather(z_pairs[1][:, 1, chunk_cols(c)], z_planes[3], z_list, z_wgt, chunk_cols(c))
+            weave_z_pair(1, c)
+
+        def make_gate(h, codes_tag=None):
+            gate = sb("gate%d" % h, [P, PLANES, HALF], F32)
+            for i, bank in enumerate(project(wb, "z%d" % h, z_woven[h][:], HALF, codes_tag)):
+                nc.scalar.activation(gate[:, i, :], bank[:, 0, :], ACT.Sigmoid)
+            return gate
+
+        gates = [make_gate(0)]
+        wa = deal_weight("wa", wa_word_tile, wa_scale_tile)
+
+        x_picked = [sb("x_picked%d" % c, [P, PLANES, CHUNK], F32) for c in range(CHUNKS)]
+
+        def gather_x(i, c):
+            gather(x_picked[c][:, i, :], x_planes[i], x_list, x_wgt, chunk_cols(c))
+
+        for c in range(CHUNKS):
+            gather_x(0, c)
+        gates.append(make_gate(1, "x_plane0"))
+        for c in range(CHUNKS):
+            gather_x(1, c)
+
+        def gather_x_late_planes(c):
+            for i in range(2, PLANES):
+                gather_x(i, c)
+
+        def project_x(c, woven):
+            weave(nc.scalar.copy, woven, x_picked[c][:])
+            return project(wa, "x%d" % c, woven, CHUNK)
+
+        for c in range(LAST):
+            gather_x_late_planes(c)
+        ya_banks = [project_x(0, x_picked[LAST][:, 2:, :].rearrange("p i j -> p (i j)").bitcast(BF16))]
+        gather_x_late_planes(LAST)
 
         y_scales = sb("y_scales", [P, J], U8)
-        ov = out_0.rearrange("(p i) j -> p i j", i=PACK)
-        def pick(c):
-            j0, j1 = spans[c]
-            for i in range(2, PACK):
-                gather(xg[c][:, i, :], x_rows[i], x_list, x_wgt, j0, j1)
-
-        def stage1(c):
-            j0, j1 = spans[c]
-            if c in late:
-                xb = xg[c + 2][:, late[c] :, :].rearrange("p i j -> p (i j)")[:, : 2 * (j1 - j0)].bitcast(BF16)
-            else:
-                xb = sb("xb%d" % c, [P, PACK * (j1 - j0)], BF16)[:]
-            weave(nc.scalar.copy, xb, xg[c][:, :PACK, :])
-            banks = project(wa, "x%d" % c, xb, j1 - j0)
-            if c + 2 < len(spans):
-                pick(c + 2)
-            return banks
-
-        pick(0)
-        pick(1)
-        for c, (j0, j1) in enumerate(spans):
-            width = j1 - j0
-            cols = slice(j0, j1)
-            banks = stage1(c)
-            prod = sb("prod%d" % c, [P, PACK, width], F32)
-            per_bank = PACK // len(banks)
-            for h, bank in enumerate(banks):
-                rows = slice(per_bank * h, per_bank * (h + 1))
-                nc.vector.tensor_tensor(prod[:, rows, :], bank[:], gate[j0 // (2 * C)][:, rows, j0 % (2 * C) : j0 % (2 * C) + width], MULT)
-            y = sb("y%d" % c, [P, PACK, width], F32)
-            for i in range(PACK):
-                if c in (3,):
-                    nc.vector.tensor_scalar_add(y[:, i, :], prod[:, i, :], bias[:, i : i + 1])
+        y_hbm = out_0.rearrange("(p i) j -> p i j", i=PLANES)
+        codes_hbm = out_1[0].rearrange("p j i -> p (j i)").bitcast(I32)
+        for c in range(CHUNKS):
+            if c < LAST:
+                ya_banks.append(project_x(c + 1, sb("x_woven%d" % (c + 1), [P, PLANES * CHUNK], BF16)[:]))
+            gated = sb("gated%d" % c, [P, PLANES, CHUNK], F32)
+            gate_start = CHUNK * c % HALF
+            per_bank = BANK_COLS // CHUNK
+            for h, bank in enumerate(ya_banks[c]):
+                planes = slice(per_bank * h, per_bank * (h + 1))
+                gate = gates[CHUNK * c // HALF][:, planes, gate_start : gate_start + CHUNK]
+                nc.vector.tensor_tensor(gated[:, planes, :], bank[:], gate, MULT)
+            y = sb("y%d" % c, [P, PLANES, CHUNK], F32)
+            for i in range(PLANES):
+                if c in BIAS_ON_VECTOR:
+                    nc.vector.tensor_scalar_add(y[:, i, :], gated[:, i, :], bias[:, i : i + 1])
                 else:
-                    nc.scalar.activation(y[:, i, :], prod[:, i, :], ACT.Identity, bias=bias[:, i : i + 1])
-            nc.sync.dma_start(ov[:, :, cols], y[:])
-            yb = sb("yb%d" % c, [P, PACK * width], BF16)
-            weave(nc.scalar.copy if c in WEAVE_ON_SCALAR else nc.vector.tensor_copy, yb, y[:])
-            y_codes = sb("y_codes%d" % c, [P, width], U32)
-            nc.vector.quantize_mx(out=y_codes[:].bitcast(FP8X4), scales=y_scales[:, cols], in_=yb[:])
-            nc.sync.dma_start(
-                out_1[0].rearrange("p j i -> p (j i)")[:, PACK * j0 : PACK * j1].bitcast(I32),
-                y_codes[:].bitcast(I32),
-            )
-        for q in range(4):
+                    nc.scalar.activation(y[:, i, :], gated[:, i, :], ACT.Identity, bias=bias[:, i : i + 1])
+            nc.sync.dma_start(y_hbm[:, :, chunk_cols(c)], y[:])
+            y_woven = sb("y_woven%d" % c, [P, PLANES * CHUNK], BF16)
+            weave(nc.vector.tensor_copy if c in Y_WOVEN_ON_VECTOR else nc.scalar.copy, y_woven[:], y[:])
+            y_codes = sb("y_codes%d" % c, [P, CHUNK], U32)
+            nc.vector.quantize_mx(out=y_codes[:].bitcast(FP8X4), scales=y_scales[:, chunk_cols(c)], in_=y_woven[:])
+            nc.sync.dma_start(codes_hbm[:, chunk_cols(c)], y_codes[:].bitcast(I32))
+        for q in range(QUADRANTS):
             queue = nc.sync if q % 2 == 0 else nc.scalar
             queue.dma_start(out_2[0, 4 * q : 4 * q + 4, :].bitcast(I32), y_scales[32 * q : 32 * q + 4, :].bitcast(I32))

from contextlib import ExitStack

import concourse.mybir as mybir

K, N, T, J = 512, 512, 2048, 1024
FLOPS = 2 * 2 * K * N * J

F32 = mybir.dt.float32
BF16 = mybir.dt.bfloat16
I32 = mybir.dt.int32
U32 = mybir.dt.uint32
U16 = mybir.dt.uint16
U8 = mybir.dt.uint8
FP8X4 = mybir.dt.float8_e4m3fn_x4
FP4X4 = mybir.dt.float4_e2m1fn_x4
MULT = mybir.AluOpType.mult
ACT = mybir.ActivationFunctionType

P = 128
PLANES = 4
LIST_ROWS = 16
QUADRANTS = 4
BANKS = 8
BANK_COLS = 512
RUN = 4
CHUNK = 256
CHUNKS = J // CHUNK
HALF = J // 2
LAST = CHUNKS - 1
Y_WOVEN_ON_VECTOR = (0, LAST)
BIAS_ON_VECTOR = (LAST,)


def tile_list_gate_biasP_kernel(
    tc, xT, wgt, zT, wgt2, wa_words, wa_scales, wb_words, wb_scales, b, offs, offs2, out_0, out_1, out_2
):
    nc = tc.nc
    with ExitStack() as ctx:
        keep = ctx.enter_context(tc.tile_pool(name="keep", bufs=1))
        psum = ctx.enter_context(tc.psum_pool(name="psum", bufs=BANKS))

        def sb(name, shape, dtype, tag=None):
            return keep.tile(shape, dtype, name=name, tag=tag or name, align_bytes=64)

        x_list = keep.tile([P, J // LIST_ROWS], U16, name="x_list")
        z_list = keep.tile([P, J // LIST_ROWS], U16, name="z_list")
        x_wgt = sb("x_wgt", [P, J], F32)
        z_wgt = sb("z_wgt", [P, J], F32)
        x_planes = [sb("x_plane%d" % i, [P, T], F32) for i in range(PLANES)]
        z_planes = [sb("z_plane%d" % i, [P, T], F32) for i in range(PLANES)]
        x_hbm = xT.rearrange("(p i) t -> i p t", i=PLANES)
        z_hbm = zT.rearrange("(p i) t -> i p t", i=PLANES)
        bias = sb("bias", [P, PLANES], F32)

        def cleared_scale_tile(name):
            scale_tile = sb(name, [P, N], U8)
            nc.gpsimd.memset(scale_tile[:].bitcast(I32), 0)
            return scale_tile

        def load_scales(scale_tile, scales, quadrants):
            for q in quadrants:
                nc.sync.dma_start(
                    scale_tile[32 * q : 32 * q + 4, :].bitcast(I32), scales[0, 4 * q : 4 * q + 4, :].bitcast(I32)
                )

        def load_words(name, words):
            word_tile = sb(name, [P, 2 * N], U8)
            nc.sync.dma_start(word_tile[:].bitcast(I32), words[0].bitcast(I32))
            return word_tile

        def deal_weight(name, word_tile, scale_tile):
            words = sb(name + "_words", [P, 2 * N], U8)
            scales = sb(name + "_scales", [P, N], U8)
            nc.vector.tensor_copy(
                words[:].bitcast(U16).rearrange("p (i m) -> p i m", i=PLANES),
                word_tile[:].bitcast(U16).rearrange("p (m i) -> p i m", i=PLANES),
            )
            nc.vector.tensor_copy(
                scales[:].rearrange("p (i m) -> p i m", i=PLANES), scale_tile[:].rearrange("p (m i) -> p i m", i=PLANES)
            )
            return words, scales

        wb_scale_tile = cleared_scale_tile("wb_loaded_scales")
        wa_scale_tile = cleared_scale_tile("wa_loaded_scales")
        nc.sync.dma_start(z_planes[0][:], z_hbm[0])
        nc.sync.dma_start(z_list[:], offs2)
        nc.sync.dma_start(z_wgt[:, :CHUNK], wgt2[:, :CHUNK])
        nc.sync.dma_start(z_wgt[:, CHUNK:], wgt2[:, CHUNK:])
        nc.sync.dma_start(z_planes[1][:], z_hbm[1])
        wb_word_tile = load_words("wb_loaded_words", wb_words)
        load_scales(wb_scale_tile, wb_scales, (0, 1))
        nc.sync.dma_start(z_planes[2][:], z_hbm[2])
        load_scales(wb_scale_tile, wb_scales, (2, 3))
        nc.sync.dma_start(z_planes[3][:], z_hbm[3])
        nc.sync.dma_start(x_list[:], offs)
        nc.sync.dma_start(x_wgt[:], wgt)
        nc.sync.dma_start(x_planes[0][:], x_hbm[0])
        wa_word_tile = load_words("wa_loaded_words", wa_words)
        load_scales(wa_scale_tile, wa_scales, (0, 1))
        nc.sync.dma_start(x_planes[1][:], x_hbm[1])
        load_scales(wa_scale_tile, wa_scales, (2, 3))
        nc.sync.dma_start(x_planes[2][:], x_hbm[2])
        nc.sync.dma_start(bias[:], b.rearrange("(p i) -> p i", i=PLANES))
        nc.sync.dma_start(x_planes[3][:], x_hbm[3])
        wb = deal_weight("wb", wb_word_tile, wb_scale_tile)

        def chunk_cols(c):
            return slice(CHUNK * c, CHUNK * (c + 1))

        def gather(dst, plane, offsets, weights, cols):
            picked = plane[:].indirect(offsets[:, cols.start // LIST_ROWS : cols.stop // LIST_ROWS])
            nc.vector.tensor_tensor(dst, picked, weights[:, cols], MULT)

        def weave(engine_copy, dst, src, planes=slice(0, PLANES)):
            engine_copy(
                dst.rearrange("p (c u i) -> p c i u", u=RUN, i=PLANES)[:, :, planes, :],
                src.rearrange("p i (c u) -> p c i u", u=RUN),
            )

        def project(weight, name, woven, width, codes_tag=None):
            w_words, w_scales = weight
            codes = sb(name + "_codes", [P, width], U32, codes_tag)
            scales = sb(name + "_scales", [P, width], U8)
            nc.vector.quantize_mx(out=codes[:].bitcast(FP8X4), scales=scales[:], in_=woven)
            banks = []
            per_bank = BANK_COLS // width
            for first in range(0, PLANES, per_bank):
                bank = psum.tile([P, per_bank, width], F32, name="bank")
                for e in range(per_bank):
                    col = P * (first + e)
                    nc.tensor.matmul_mx(
                        out=bank[:, e, :],
                        lhsT=w_words[:, 2 * col : 2 * (col + P)].bitcast(FP4X4),
                        lhsT_scale=w_scales[:, col : col + P],
                        rhs=codes[:].bitcast(FP8X4),
                        rhs_scale=scales[:],
                        start=True,
                        stop=True,
                    )
                banks.append(bank)
            return banks

        z_pairs = [sb("z_pair%d" % h, [P, 2, J], F32) for h in range(2)]
        z_woven = [sb("z_woven%d" % h, [P, PLANES * HALF], BF16) for h in range(2)]

        def weave_z_pair(pair, c):
            start = PLANES * (CHUNK * c % HALF)
            dst = z_woven[CHUNK * c // HALF][:, start : start + PLANES * CHUNK]
            weave(nc.scalar.copy, dst, z_pairs[pair][:, :, chunk_cols(c)], slice(2 * pair, 2 * pair + 2))

        gather(z_pairs[0][:, 0, :CHUNK], z_planes[0], z_list, z_wgt, slice(0, CHUNK))
        gather(z_pairs[0][:, 0, CHUNK:], z_planes[0], z_list, z_wgt, slice(CHUNK, J))
        gather(z_pairs[0][:, 1, :], z_planes[1], z_list, z_wgt, slice(0, J))
        for c in range(CHUNKS):
            weave_z_pair(0, c)
        gather(z_pairs[1][:, 0, :], z_planes[2], z_list, z_wgt, slice(0, J))
        for c in range(CHUNKS):
            gather(z_pairs[1][:, 1, chunk_cols(c)], z_planes[3], z_list, z_wgt, chunk_cols(c))
            weave_z_pair(1, c)

        def make_gate(h, codes_tag=None):
            gate = sb("gate%d" % h, [P, PLANES, HALF], F32)
            for i, bank in enumerate(project(wb, "z%d" % h, z_woven[h][:], HALF, codes_tag)):
                nc.scalar.activation(gate[:, i, :], bank[:, 0, :], ACT.Sigmoid)
            return gate

        gates = [make_gate(0)]
        wa = deal_weight("wa", wa_word_tile, wa_scale_tile)

        x_picked = [sb("x_picked%d" % c, [P, PLANES, CHUNK], F32) for c in range(CHUNKS)]

        def gather_x(i, c):
            gather(x_picked[c][:, i, :], x_planes[i], x_list, x_wgt, chunk_cols(c))

        for c in range(CHUNKS):
            gather_x(0, c)
        gates.append(make_gate(1, "x_plane0"))
        for c in range(CHUNKS):
            gather_x(1, c)

        def gather_x_late_planes(c):
            for i in range(2, PLANES):
                gather_x(i, c)

        def project_x(c, woven):
            weave(nc.scalar.copy, woven, x_picked[c][:])
            return project(wa, "x%d" % c, woven, CHUNK)

        for c in range(LAST):
            gather_x_late_planes(c)
        ya_banks = [project_x(0, x_picked[LAST][:, 2:, :].rearrange("p i j -> p (i j)").bitcast(BF16))]
        gather_x_late_planes(LAST)

        y_scales = sb("y_scales", [P, J], U8)
        y_hbm = out_0.rearrange("(p i) j -> p i j", i=PLANES)
        codes_hbm = out_1[0].rearrange("p j i -> p (j i)").bitcast(I32)
        for c in range(CHUNKS):
            if c < LAST:
                ya_banks.append(project_x(c + 1, sb("x_woven%d" % (c + 1), [P, PLANES * CHUNK], BF16)[:]))
            gated = sb("gated%d" % c, [P, PLANES, CHUNK], F32)
            gate_start = CHUNK * c % HALF
            per_bank = BANK_COLS // CHUNK
            for h, bank in enumerate(ya_banks[c]):
                planes = slice(per_bank * h, per_bank * (h + 1))
                gate = gates[CHUNK * c // HALF][:, planes, gate_start : gate_start + CHUNK]
                nc.vector.tensor_tensor(gated[:, planes, :], bank[:], gate, MULT)
            y = sb("y%d" % c, [P, PLANES, CHUNK], F32)
            for i in range(PLANES):
                if c in BIAS_ON_VECTOR:
                    nc.vector.tensor_scalar_add(y[:, i, :], gated[:, i, :], bias[:, i : i + 1])
                else:
                    nc.scalar.activation(y[:, i, :], gated[:, i, :], ACT.Identity, bias=bias[:, i : i + 1])
            nc.sync.dma_start(y_hbm[:, :, chunk_cols(c)], y[:])
            y_woven = sb("y_woven%d" % c, [P, PLANES * CHUNK], BF16)
            weave(nc.vector.tensor_copy if c in Y_WOVEN_ON_VECTOR else nc.scalar.copy, y_woven[:], y[:])
            y_codes = sb("y_codes%d" % c, [P, CHUNK], U32)
            nc.vector.quantize_mx(out=y_codes[:].bitcast(FP8X4), scales=y_scales[:, chunk_cols(c)], in_=y_woven[:])
            nc.sync.dma_start(codes_hbm[:, chunk_cols(c)], y_codes[:].bitcast(I32))
        for q in range(QUADRANTS):
            queue = nc.sync if q % 2 == 0 else nc.scalar
            queue.dma_start(out_2[0, 4 * q : 4 * q + 4, :].bitcast(I32), y_scales[32 * q : 32 * q + 4, :].bitcast(I32))
